import numpy as np
import ml_dtypes


def mxq(x, axis, fmt="e4m3"):
    dtype, down = {"e4m3": (ml_dtypes.float8_e4m3fn, 7), "e5m2": (ml_dtypes.float8_e5m2, 14)}[fmt]
    v = np.moveaxis(np.asarray(x, np.float32).astype(ml_dtypes.bfloat16).astype(np.float64), axis, -1)
    blocks = v.reshape(v.shape[:-1] + (-1, 32))
    amax = np.abs(blocks).max(-1, keepdims=True)
    byte = np.maximum(np.where(amax > 0, np.frexp(amax)[1] - 1 + 127, 0) - down, 1)
    scale = np.exp2(byte - 127.0)
    codes = (blocks / scale).astype(np.float32).astype(dtype).astype(np.float64)
    return np.moveaxis((codes * scale).reshape(v.shape), -1, axis)


WIDE = False


def mx_kscale(k):
    if not WIDE:
        return np.ones(k)
    levels = np.array([10, -10, 5, -5, 0])
    if k % 512:
        return np.exp2(np.random.permutation(np.resize(levels, k // 32))).repeat(32)
    a = np.empty((k // 512, 16))
    for p in range(k // 512):
        a[p, :8] = np.random.permutation(np.resize(levels, 8))
        for g in range(8):
            far = levels[np.abs(levels - a[p, g]) >= 10]
            a[p, g + 8] = far[np.random.randint(len(far))]
    return np.exp2(a.ravel()).repeat(32)


def f64(x):
    return np.asarray(x).astype(np.float64)


def striped(idx):
    return np.tile(idx.reshape(-1, 16).T, (8, 1)).astype(np.uint16)


def unstriped(offs):
    return offs[:16].T.reshape(-1).astype(np.int64)


def pack_weight(w):
    k, n = w.shape
    w = f64(np.asarray(w, np.float32).astype(ml_dtypes.bfloat16)).reshape(k // 32, 32, n)
    amax = np.abs(w).max(1)
    byte = np.clip(np.where(amax > 0, np.frexp(amax)[1] - 1 + 127 - 7, 1), 1, 254)
    scaled = (w * np.exp2(127.0 - byte)[:, None, :]).reshape(k, n).astype(np.float32)
    words = np.ascontiguousarray(scaled.reshape(k // 512, 128, 4, n).transpose(0, 1, 3, 2)).astype(ml_dtypes.float8_e4m3fn).view(np.uint8)
    return words, np.ascontiguousarray(byte.astype(np.uint8).reshape(k // 512, 16, n))


def unpack_weight(words, scales):
    g, p, n, _ = words.shape
    vals = np.ascontiguousarray(words).view(ml_dtypes.float8_e4m3fn).astype(np.float64) * np.repeat(np.exp2(scales.astype(np.float64) - 127.0), 8, axis=1)[..., None]
    return vals.transpose(0, 1, 3, 2).reshape(g * 512, n)


K, T, S, N = 1024, 2048, 512, 128
P = 2 ** 7


def setup_inputs():
    n = np.random.standard_normal
    s = mx_kscale(K)[:, None]
    packed_xT = pack_weight(n((K, T)) * s)
    return {
        "x_words": packed_xT[0],
        "x_scales": packed_xT[1],
        "w1": (n((K, N)) / np.sqrt(K) / s).astype(np.float32),
        "fe": (n((N, S))).astype(np.float32),
        "fh": (n((N, S))).astype(np.float32),
        "ca": (np.tile(np.random.uniform(0.5, 0.95, S), (P, 1))).astype(np.float32),
        "da": (np.tile(np.random.uniform(0.6, 1.0, S), (P, 1))).astype(np.float32),
        "offs": striped(np.random.permutation(T)[:S]),
        "up": striped(np.random.permutation(S)),
        "dn": striped(np.random.permutation(S)),
        "lt": striped(np.random.permutation(S)),
        "rt": striped(np.random.permutation(S)),
    }


def reference(x_words, x_scales, w1, fe, fh, ca, da, offs, up, dn, lt, rt):
    curl = f64(fh)[:, unstriped(up)] - f64(fh)[:, unstriped(dn)]
    xq = unpack_weight(x_words, x_scales)[:, unstriped(offs)]
    y = mxq(f64(w1), 0, "e4m3").T @ xq
    en = f64(fe) * f64(ca)[:1] + 0.5 * curl - (0.4 * y)
    return f64(fh) * f64(da)[:1] + 0.5 * (en[:, unstriped(lt)] - en[:, unstriped(rt)])

@@ -1,0 +1,146 @@
+from contextlib import ExitStack
+
+import concourse.mybir as mybir
+from concourse.masks import make_identity
+
+K, T, S, M = 1024, 2048, 512, 128
+FLOPS = 2 * K * S * M
+
+F32 = mybir.dt.float32
+BF16 = mybir.dt.bfloat16
+I32 = mybir.dt.int32
+U32 = mybir.dt.uint32
+U16 = mybir.dt.uint16
+U8 = mybir.dt.uint8
+FP8X4 = mybir.dt.float8_e4m3fn_x4
+MULT = mybir.AluOpType.mult
+ADD = mybir.AluOpType.add
+SUB = mybir.AluOpType.subtract
+
+P = 128
+PACK = 4
+PASSES = K // (P * PACK)
+HALF = S // 2
+HALVES = 2
+
+
+def tile_picked_yfdtd_pml_p_kernel(
+    tc, x_words, x_scales, w1, fe, fh, ca, da, offs, up, dn, lt, rt, out
+):
+    nc = tc.nc
+    with ExitStack() as ctx:
+        sb = ctx.enter_context(tc.tile_pool(name="sb", bufs=1))
+        ps = ctx.enter_context(tc.psum_pool(name="ps", bufs=1))
+
+        def cols(h):
+            return slice(h * HALF, (h + 1) * HALF)
+
+        def entries(h):
+            return slice(h * HALF // 16, (h + 1) * HALF // 16)
+
+        def load_list(name, src):
+            t = sb.tile([P, S // 16], U16, name=name)
+            nc.sync.dma_start(t[:], src)
+            return t
+
+        ident = sb.tile([P, P], F32, name="ident")
+        make_identity(nc, ident[:])
+        scale_tab = sb.tile([P, T], U8, name="scale_tab", tag="scale_slot", align_bytes=64)
+        nc.vector.memset(scale_tab[:].bitcast(I32), 0)
+
+        ca_col = sb.tile([P, 4], F32, name="ca_col")
+        nc.scalar.dma_start(ca_col[:], ca[0:1, :].rearrange("o (p b) -> p (o b)", b=4))
+        fe_sb = sb.tile([P, S], F32, name="fe_sb")
+        nc.sync.dma_start(fe_sb[:], fe)
+        fh_sb = sb.tile([P, S], F32, name="fh_sb")
+        nc.sync.dma_start(fh_sb[:], fh)
+        up_sb = load_list("up_sb", up)
+        dn_sb = load_list("dn_sb", dn)
+        for q in range(4):
+            nc.gpsimd.dma_start(
+                scale_tab[32 * q : 32 * q + 8, :].bitcast(I32),
+                x_scales[:, 4 * q : 4 * q + 4, :].bitcast(I32),
+            )
+        word_tab = [sb.tile([P, T], I32, name=f"word_tab{o}", tag=f"word_slot{o}") for o in range(PASSES)]
+        w_raw = sb.tile([P, PASSES, PACK, M], F32, name="w_raw")
+        nc.sync.dma_start(w_raw[:], w1.rearrange("(o p j) m -> p o j m", o=PASSES, j=PACK))
+        nc.sync.dma_start(word_tab[0][:], x_words[0].rearrange("p n t -> p (n t)").bitcast(I32))
+        offs_sb = load_list("offs_sb", offs)
+        nc.sync.dma_start(word_tab[1][:], x_words[1].rearrange("p n t -> p (n t)").bitcast(I32))
+        da_sb = sb.tile([P, S], F32, name="da_sb")
+        nc.sync.dma_start(da_sb[:], da)
+        lt_sb = load_list("lt_sb", lt)
+        rt_sb = load_list("rt_sb", rt)
+
+        def spread(name, col):
+            rows = ps.tile([P, 4, P], F32, name=name)
+            for b in range(4):
+                nc.tensor.transpose(rows[:, b, :], col[:, b : b + 1].to_broadcast([P, P]), ident[:])
+            return rows[:].rearrange("m b p -> m p b")
+
+        def by4(ap):
+            return ap.rearrange("m (p b) -> m p b", b=4)
+
+        ca_rows = spread("ca_rows", ca_col)
+        fc = sb.tile([P, S], F32, name="fc", tag="fc_slot", align_bytes=64)
+        for h in range(HALVES):
+            nc.vector.scalar_tensor_tensor(
+                by4(fc[:, cols(h)]), by4(fe_sb[:, cols(h)]), 2.0, ca_rows[:, h * 64 : (h + 1) * 64, :], MULT, MULT
+            )
+        t1 = sb.tile([P, S], F32, name="t1", tag="t1_slot", align_bytes=64)
+        for h in range(HALVES):
+            nc.vector.tensor_tensor(t1[:, cols(h)], fh_sb[:].indirect(up_sb[:, entries(h)]), fc[:, cols(h)], ADD)
+        t2 = sb.tile([P, S], F32, name="t2")
+        for h in range(HALVES):
+            nc.vector.tensor_tensor(t2[:, cols(h)], fh_sb[:].indirect(dn_sb[:, entries(h)]), t1[:, cols(h)], SUB)
+        t2q = sb.tile([P, S], F32, name="t2q")
+        nc.scalar.mul(t2q[:], t2[:], 0.25)
+
+        w_bf = sb.tile([P, PASSES, M, PACK], BF16, name="w_bf", align_bytes=64)
+        for o in range(PASSES):
+            nc.scalar.copy(w_bf[:, o], w_raw[:, o].rearrange("p j m -> p m j"))
+        w_codes = sb.tile([P, PASSES * M], U32, name="w_codes", tag="fc_slot", align_bytes=64)
+        w_scales = sb.tile([P, PASSES * M], U8, name="w_scales", align_bytes=64)
+        nc.vector.quantize_mx(w_codes[:].bitcast(FP8X4), w_scales[:], w_bf[:].rearrange("p o m j -> p (o m j)"))
+
+        words0 = sb.tile([P, S], U32, name="words0", tag="t1_slot", align_bytes=64)
+        nc.vector.tensor_copy(words0[:], word_tab[0][:].bitcast(U32).indirect(offs_sb[:]))
+        scales = sb.tile([P, S], U8, name="scales", align_bytes=64)
+        nc.vector.tensor_copy(scales[:], scale_tab[:].indirect(offs_sb[:]))
+
+
+        words1 = sb.tile([P, S], U32, name="words1", tag="scale_slot", align_bytes=64)
+        y = [ps.tile([P, HALF], F32, name=f"y{h}") for h in range(HALVES)]
+        for h in range(HALVES):
+            nc.tensor.matmul_mx(
+                y[h][:],
+                lhsT=w_codes[:, 0:M].bitcast(FP8X4),
+                lhsT_scale=w_scales[:, 0:M],
+                rhs=words0[:, cols(h)].bitcast(FP8X4),
+                rhs_scale=scales[:, cols(h)],
+                start=True,
+                stop=False,
+            )
+        for h in range(HALVES):
+            nc.vector.tensor_copy(words1[:, cols(h)], word_tab[1][:].bitcast(U32).indirect(offs_sb[:, entries(h)]))
+            nc.tensor.matmul_mx(
+                y[h][:],
+                lhsT=w_codes[:, M : 2 * M].bitcast(FP8X4),
+                lhsT_scale=w_scales[:, M : 2 * M],
+                rhs=words1[:, cols(h)].bitcast(FP8X4),
+                rhs_scale=scales[4:P, cols(h)],
+                start=False,
+                stop=True,
+            )
+        fd = sb.tile([P, S], F32, name="fd", tag="word_slot1")
+        nc.vector.tensor_tensor(fd[:], fh_sb[:], da_sb[:], MULT)
+        hn = sb.tile([P, S], F32, name="hn")
+        for h in range(HALVES):
+            nc.vector.scalar_tensor_tensor(hn[:, cols(h)], y[h][:], 0.2, t2q[:, cols(h)], MULT, ADD)
+        u = sb.tile([P, S], F32, name="u")
+        for h in range(HALVES):
+            nc.vector.tensor_tensor(u[:, cols(h)], hn[:].indirect(lt_sb[:, entries(h)]), fd[:, cols(h)], SUB)
+        res = [sb.tile([P, HALF], F32, name=f"res{h}") for h in range(HALVES)]
+        for h in range(HALVES):
+            nc.vector.tensor_tensor(res[h][:], hn[:].indirect(rt_sb[:, entries(h)]), u[:, cols(h)], SUB)
+            nc.sync.dma_start(out[:, cols(h)], res[h][:])

@@ -49,23 +49,23 @@ def tile_picked_yfdtd_pml_p_kernel(
         nc.vector.memset(scale_tab[:].bitcast(I32), 0)
 
         ca_col = sb.tile([P, 4], F32, name="ca_col")
-        nc.scalar.dma_start(ca_col[:], ca[0:1, :].rearrange("o (p b) -> p (o b)", b=4))
+        nc.sync.dma_start(ca_col[:], ca[0:1, :].rearrange("o (p b) -> p (o b)", b=4))
         fe_sb = sb.tile([P, S], F32, name="fe_sb")
         nc.sync.dma_start(fe_sb[:], fe)
         fh_sb = sb.tile([P, S], F32, name="fh_sb")
         nc.sync.dma_start(fh_sb[:], fh)
         up_sb = load_list("up_sb", up)
         dn_sb = load_list("dn_sb", dn)
-        for q in range(4):
-            nc.gpsimd.dma_start(
-                scale_tab[32 * q : 32 * q + 8, :].bitcast(I32),
-                x_scales[:, 4 * q : 4 * q + 4, :].bitcast(I32),
-            )
         word_tab = [sb.tile([P, T], I32, name=f"word_tab{o}", tag=f"word_slot{o}") for o in range(PASSES)]
         w_raw = sb.tile([P, PASSES, PACK, M], F32, name="w_raw")
         nc.sync.dma_start(w_raw[:], w1.rearrange("(o p j) m -> p o j m", o=PASSES, j=PACK))
         nc.sync.dma_start(word_tab[0][:], x_words[0].rearrange("p n t -> p (n t)").bitcast(I32))
         offs_sb = load_list("offs_sb", offs)
+        for q in range(4):
+            nc.sync.dma_start(
+                scale_tab[32 * q : 32 * q + 8, :].bitcast(I32),
+                x_scales[:, 4 * q : 4 * q + 4, :].bitcast(I32),
+            )
         nc.sync.dma_start(word_tab[1][:], x_words[1].rearrange("p n t -> p (n t)").bitcast(I32))
         da_sb = sb.tile([P, S], F32, name="da_sb")
         nc.sync.dma_start(da_sb[:], da)
@@ -93,7 +93,7 @@ def tile_picked_yfdtd_pml_p_kernel(
         t2 = sb.tile([P, S], F32, name="t2")
         for h in range(HALVES):
             nc.vector.tensor_tensor(t2[:, cols(h)], fh_sb[:].indirect(dn_sb[:, entries(h)]), t1[:, cols(h)], SUB)
-        t2q = sb.tile([P, S], F32, name="t2q")
+        t2q = sb.tile([P, S], F32, name="t2q", tag="t2q_slot")
         nc.scalar.mul(t2q[:], t2[:], 0.25)
 
         w_bf = sb.tile([P, PASSES, M, PACK], BF16, name="w_bf", align_bytes=64)
@@ -132,14 +132,15 @@ def tile_picked_yfdtd_pml_p_kernel(
                 start=False,
                 stop=True,
             )
-        fd = sb.tile([P, S], F32, name="fd", tag="word_slot1")
-        nc.vector.tensor_tensor(fd[:], fh_sb[:], da_sb[:], MULT)
+        fd = [sb.tile([P, HALF], F32, name="fd0", tag="word_slot1"), sb.tile([P, HALF], F32, name="fd1", tag="t2q_slot")]
+        nc.vector.tensor_tensor(fd[0][:], fh_sb[:, cols(0)], da_sb[:, cols(0)], MULT)
         hn = sb.tile([P, S], F32, name="hn")
         for h in range(HALVES):
             nc.vector.scalar_tensor_tensor(hn[:, cols(h)], y[h][:], 0.2, t2q[:, cols(h)], MULT, ADD)
+        nc.vector.tensor_tensor(fd[1][:], fh_sb[:, cols(1)], da_sb[:, cols(1)], MULT)
         u = sb.tile([P, S], F32, name="u")
         for h in range(HALVES):
-            nc.vector.tensor_tensor(u[:, cols(h)], hn[:].indirect(lt_sb[:, entries(h)]), fd[:, cols(h)], SUB)
+            nc.vector.tensor_tensor(u[:, cols(h)], hn[:].indirect(lt_sb[:, entries(h)]), fd[h][:], SUB)
         res = [sb.tile([P, HALF], F32, name=f"res{h}") for h in range(HALVES)]
         for h in range(HALVES):
             nc.vector.tensor_tensor(res[h][:], hn[:].indirect(rt_sb[:, entries(h)]), u[:, cols(h)], SUB)

@@ -16,6 +16,7 @@ FP8X4 = mybir.dt.float8_e4m3fn_x4
 MULT = mybir.AluOpType.mult
 ADD = mybir.AluOpType.add
 SUB = mybir.AluOpType.subtract
+COPY = mybir.ActivationFunctionType.Copy
 
 P = 128
 PACK = 4
@@ -48,19 +49,19 @@ def tile_picked_yfdtd_pml_p_kernel(
         scale_tab = sb.tile([P, T], U8, name="scale_tab", tag="scale_slot", align_bytes=64)
         nc.vector.memset(scale_tab[:].bitcast(I32), 0)
 
-        ca_col = sb.tile([P, 4], F32, name="ca_col")
-        nc.sync.dma_start(ca_col[:], ca[0:1, :].rearrange("o (p b) -> p (o b)", b=4))
-        fe_sb = sb.tile([P, S], F32, name="fe_sb")
-        nc.sync.dma_start(fe_sb[:], fe)
         fh_sb = sb.tile([P, S], F32, name="fh_sb")
         nc.sync.dma_start(fh_sb[:], fh)
         up_sb = load_list("up_sb", up)
         dn_sb = load_list("dn_sb", dn)
+        offs_sb = load_list("offs_sb", offs)
+        ca_col = sb.tile([P, 4], F32, name="ca_col")
+        nc.sync.dma_start(ca_col[:], ca[0:1, :].rearrange("o (p b) -> p (o b)", b=4))
         word_tab = [sb.tile([P, T], I32, name=f"word_tab{o}", tag=f"word_slot{o}") for o in range(PASSES)]
+        nc.sync.dma_start(word_tab[0][:], x_words[0].rearrange("p n t -> p (n t)").bitcast(I32))
+        fe_sb = sb.tile([P, S], F32, name="fe_sb")
+        nc.sync.dma_start(fe_sb[:], fe)
         w_raw = sb.tile([P, PASSES, PACK, M], F32, name="w_raw")
         nc.sync.dma_start(w_raw[:], w1.rearrange("(o p j) m -> p o j m", o=PASSES, j=PACK))
-        nc.sync.dma_start(word_tab[0][:], x_words[0].rearrange("p n t -> p (n t)").bitcast(I32))
-        offs_sb = load_list("offs_sb", offs)
         for q in range(4):
             nc.sync.dma_start(
                 scale_tab[32 * q : 32 * q + 8, :].bitcast(I32),
@@ -72,44 +73,46 @@ def tile_picked_yfdtd_pml_p_kernel(
         lt_sb = load_list("lt_sb", lt)
         rt_sb = load_list("rt_sb", rt)
 
-        def spread(name, col):
-            rows = ps.tile([P, 4, P], F32, name=name)
-            for b in range(4):
-                nc.tensor.transpose(rows[:, b, :], col[:, b : b + 1].to_broadcast([P, P]), ident[:])
-            return rows[:].rearrange("m b p -> m p b")
-
-        def by4(ap):
-            return ap.rearrange("m (p b) -> m p b", b=4)
-
-        ca_rows = spread("ca_rows", ca_col)
-        fc = sb.tile([P, S], F32, name="fc", tag="fc_slot", align_bytes=64)
-        for h in range(HALVES):
-            nc.vector.scalar_tensor_tensor(
-                by4(fc[:, cols(h)]), by4(fe_sb[:, cols(h)]), 2.0, ca_rows[:, h * 64 : (h + 1) * 64, :], MULT, MULT
-            )
         t1 = sb.tile([P, S], F32, name="t1", tag="t1_slot", align_bytes=64)
         for h in range(HALVES):
-            nc.vector.tensor_tensor(t1[:, cols(h)], fh_sb[:].indirect(up_sb[:, entries(h)]), fc[:, cols(h)], ADD)
+            nc.vector.tensor_copy(t1[:, cols(h)], fh_sb[:].indirect(up_sb[:, entries(h)]))
         t2 = sb.tile([P, S], F32, name="t2")
         for h in range(HALVES):
             nc.vector.tensor_tensor(t2[:, cols(h)], fh_sb[:].indirect(dn_sb[:, entries(h)]), t1[:, cols(h)], SUB)
-        t2q = sb.tile([P, S], F32, name="t2q", tag="t2q_slot")
-        nc.scalar.mul(t2q[:], t2[:], 0.25)
 
-        w_bf = sb.tile([P, PASSES, M, PACK], BF16, name="w_bf", align_bytes=64)
-        for o in range(PASSES):
-            nc.scalar.copy(w_bf[:, o], w_raw[:, o].rearrange("p j m -> p m j"))
-        w_codes = sb.tile([P, PASSES * M], U32, name="w_codes", tag="fc_slot", align_bytes=64)
-        w_scales = sb.tile([P, PASSES * M], U8, name="w_scales", align_bytes=64)
-        nc.vector.quantize_mx(w_codes[:].bitcast(FP8X4), w_scales[:], w_bf[:].rearrange("p o m j -> p (o m j)"))
+        def turn(name, src):
+            turned = ps.tile([P, 4, P], F32, name=name)
+            for b in range(4):
+                nc.tensor.transpose(turned[:, b, :], src[:, b : S : 4], ident[:])
+            return turned
+
+        t2_ps = turn("t2_ps", t2)
+        t2_t = sb.tile([P, 4, P], F32, name="t2_t")
+        nc.scalar.mul(t2_t[:], t2_ps[:], -0.5)
+        fe_ps = turn("fe_ps", fe_sb)
+        fc_t = sb.tile([P, 4, P], F32, name="fc_t")
+        for b in range(4):
+            nc.scalar.activation(fc_t[:, b, :], fe_ps[:, b, :], COPY, scale=ca_col[:, b : b + 1])
+        sum_ps = ps.tile([P, 4, P], F32, name="sum_ps")
+        for b in range(4):
+            nc.tensor.matmul(sum_ps[:, b, :], lhsT=t2_t[:, b, :], rhs=ident[:], start=True, stop=False, is_transpose=True)
+            nc.tensor.matmul(sum_ps[:, b, :], lhsT=fc_t[:, b, :], rhs=ident[:], start=False, stop=True, is_transpose=True)
+        t2q = sb.tile([P, S], F32, name="t2q", tag="t2q_slot")
+        nc.scalar.mul(t2q[:].rearrange("m (p b) -> m p b", b=4), sum_ps[:].rearrange("m b p -> m p b"), -0.5)
 
         words0 = sb.tile([P, S], U32, name="words0", tag="t1_slot", align_bytes=64)
         nc.vector.tensor_copy(words0[:], word_tab[0][:].bitcast(U32).indirect(offs_sb[:]))
         scales = sb.tile([P, S], U8, name="scales", align_bytes=64)
         nc.vector.tensor_copy(scales[:], scale_tab[:].indirect(offs_sb[:]))
 
+        w_bf = sb.tile([P, PASSES, M, PACK], BF16, name="w_bf", tag="w_bf_slot", align_bytes=64)
+        for o in range(PASSES):
+            nc.scalar.copy(w_bf[:, o], w_raw[:, o].rearrange("p j m -> p m j"))
+        w_codes = sb.tile([P, PASSES * M], U32, name="w_codes", tag="scale_slot", align_bytes=64)
+        w_scales = sb.tile([P, PASSES * M], U8, name="w_scales", align_bytes=64)
+        nc.vector.quantize_mx(w_codes[:].bitcast(FP8X4), w_scales[:], w_bf[:].rearrange("p o m j -> p (o m j)"))
 
-        words1 = sb.tile([P, S], U32, name="words1", tag="scale_slot", align_bytes=64)
+        words1 = sb.tile([P, S], U32, name="words1", tag="w_bf_slot", align_bytes=64)
         y = [ps.tile([P, HALF], F32, name=f"y{h}") for h in range(HALVES)]
         for h in range(HALVES):
             nc.tensor.matmul_mx(

@@ -56,10 +56,10 @@ def tile_picked_yfdtd_pml_p_kernel(
         offs_sb = load_list("offs_sb", offs)
         ca_col = sb.tile([P, 4], F32, name="ca_col")
         nc.sync.dma_start(ca_col[:], ca[0:1, :].rearrange("o (p b) -> p (o b)", b=4))
-        word_tab = [sb.tile([P, T], I32, name=f"word_tab{o}", tag=f"word_slot{o}") for o in range(PASSES)]
-        nc.sync.dma_start(word_tab[0][:], x_words[0].rearrange("p n t -> p (n t)").bitcast(I32))
         fe_sb = sb.tile([P, S], F32, name="fe_sb")
         nc.sync.dma_start(fe_sb[:], fe)
+        word_tab = [sb.tile([P, T], I32, name=f"word_tab{o}", tag=f"word_slot{o}") for o in range(PASSES)]
+        nc.sync.dma_start(word_tab[0][:], x_words[0].rearrange("p n t -> p (n t)").bitcast(I32))
         w_raw = sb.tile([P, PASSES, PACK, M], F32, name="w_raw")
         nc.sync.dma_start(w_raw[:], w1.rearrange("(o p j) m -> p o j m", o=PASSES, j=PACK))
         for q in range(4):
@@ -76,7 +76,7 @@ def tile_picked_yfdtd_pml_p_kernel(
         t1 = sb.tile([P, S], F32, name="t1", tag="t1_slot", align_bytes=64)
         for h in range(HALVES):
             nc.vector.tensor_copy(t1[:, cols(h)], fh_sb[:].indirect(up_sb[:, entries(h)]))
-        t2 = sb.tile([P, S], F32, name="t2")
+        t2 = sb.tile([P, S], F32, name="t2", tag="w_bf_slot", align_bytes=64)
         for h in range(HALVES):
             nc.vector.tensor_tensor(t2[:, cols(h)], fh_sb[:].indirect(dn_sb[:, entries(h)]), t1[:, cols(h)], SUB)
 
@@ -86,18 +86,18 @@ def tile_picked_yfdtd_pml_p_kernel(
                 nc.tensor.transpose(turned[:, b, :], src[:, b : S : 4], ident[:])
             return turned
 
-        t2_ps = turn("t2_ps", t2)
-        t2_t = sb.tile([P, 4, P], F32, name="t2_t")
-        nc.scalar.mul(t2_t[:], t2_ps[:], -0.5)
         fe_ps = turn("fe_ps", fe_sb)
         fc_t = sb.tile([P, 4, P], F32, name="fc_t")
         for b in range(4):
             nc.scalar.activation(fc_t[:, b, :], fe_ps[:, b, :], COPY, scale=ca_col[:, b : b + 1])
+        t2_ps = turn("t2_ps", t2)
+        t2_t = sb.tile([P, 4, P], F32, name="t2_t")
+        nc.scalar.mul(t2_t[:], t2_ps[:], -0.5)
         sum_ps = ps.tile([P, 4, P], F32, name="sum_ps")
         for b in range(4):
             nc.tensor.matmul(sum_ps[:, b, :], lhsT=t2_t[:, b, :], rhs=ident[:], start=True, stop=False, is_transpose=True)
             nc.tensor.matmul(sum_ps[:, b, :], lhsT=fc_t[:, b, :], rhs=ident[:], start=False, stop=True, is_transpose=True)
-        t2q = sb.tile([P, S], F32, name="t2q", tag="t2q_slot")
+        t2q = sb.tile([P, S], F32, name="t2q")
         nc.scalar.mul(t2q[:].rearrange("m (p b) -> m p b", b=4), sum_ps[:].rearrange("m b p -> m p b"), -0.5)
 
         words0 = sb.tile([P, S], U32, name="words0", tag="t1_slot", align_bytes=64)
@@ -135,12 +135,14 @@ def tile_picked_yfdtd_pml_p_kernel(
                 start=False,
                 stop=True,
             )
-        fd = [sb.tile([P, HALF], F32, name="fd0", tag="word_slot1"), sb.tile([P, HALF], F32, name="fd1", tag="t2q_slot")]
-        nc.vector.tensor_tensor(fd[0][:], fh_sb[:, cols(0)], da_sb[:, cols(0)], MULT)
+        fd = [
+            sb.tile([P, HALF], F32, name="fd0", tag="word_slot1"),
+            sb.tile([P, HALF], F32, name="fd1", tag="w_bf_slot", align_bytes=64),
+        ]
         hn = sb.tile([P, S], F32, name="hn")
         for h in range(HALVES):
             nc.vector.scalar_tensor_tensor(hn[:, cols(h)], y[h][:], 0.2, t2q[:, cols(h)], MULT, ADD)
-        nc.vector.tensor_tensor(fd[1][:], fh_sb[:, cols(1)], da_sb[:, cols(1)], MULT)
+            nc.vector.tensor_tensor(fd[h][:], fh_sb[:, cols(h)], da_sb[:, cols(h)], MULT)
         u = sb.tile([P, S], F32, name="u")
         for h in range(HALVES):
             nc.vector.tensor_tensor(u[:, cols(h)], hn[:].indirect(lt_sb[:, entries(h)]), fd[h][:], SUB)

from contextlib import ExitStack

import concourse.mybir as mybir
from concourse.masks import make_identity

K, T, S, M = 1024, 2048, 512, 128
FLOPS = 2 * K * S * M

F32 = mybir.dt.float32
BF16 = mybir.dt.bfloat16
I32 = mybir.dt.int32
U32 = mybir.dt.uint32
U16 = mybir.dt.uint16
U8 = mybir.dt.uint8
FP8X4 = mybir.dt.float8_e4m3fn_x4
MULT = mybir.AluOpType.mult
ADD = mybir.AluOpType.add
SUB = mybir.AluOpType.subtract
COPY = mybir.ActivationFunctionType.Copy

P = 128
PACK = 4
PASSES = K // (P * PACK)
HALF = S // 2
HALVES = 2


def tile_picked_yfdtd_pml_p_kernel(
    tc, x_words, x_scales, w1, fe, fh, ca, da, offs, up, dn, lt, rt, out
):
    nc = tc.nc
    with ExitStack() as ctx:
        sb = ctx.enter_context(tc.tile_pool(name="sb", bufs=1))
        ps = ctx.enter_context(tc.psum_pool(name="ps", bufs=1))

        def cols(h):
            return slice(h * HALF, (h + 1) * HALF)

        def entries(h):
            return slice(h * HALF // 16, (h + 1) * HALF // 16)

        def load_list(name, src):
            t = sb.tile([P, S // 16], U16, name=name)
            nc.sync.dma_start(t[:], src)
            return t

        ident = sb.tile([P, P], F32, name="ident")
        make_identity(nc, ident[:])
        scale_tab = sb.tile([P, T], U8, name="scale_tab", tag="scale_slot", align_bytes=64)
        nc.vector.memset(scale_tab[:].bitcast(I32), 0)

        fh_sb = sb.tile([P, S], F32, name="fh_sb")
        nc.sync.dma_start(fh_sb[:], fh)
        up_sb = load_list("up_sb", up)
        dn_sb = load_list("dn_sb", dn)
        offs_sb = load_list("offs_sb", offs)
        ca_col = sb.tile([P, 4], F32, name="ca_col")
        nc.sync.dma_start(ca_col[:], ca[0:1, :].rearrange("o (p b) -> p (o b)", b=4))
        fe_sb = sb.tile([P, S], F32, name="fe_sb")
        nc.sync.dma_start(fe_sb[:], fe)
        word_tab = [sb.tile([P, T], I32, name=f"word_tab{o}", tag=f"word_slot{o}") for o in range(PASSES)]
        nc.sync.dma_start(word_tab[0][:], x_words[0].rearrange("p n t -> p (n t)").bitcast(I32))
        w_raw = sb.tile([P, PASSES, PACK, M], F32, name="w_raw")
        nc.sync.dma_start(w_raw[:], w1.rearrange("(o p j) m -> p o j m", o=PASSES, j=PACK))
        for q in range(4):
            nc.sync.dma_start(
                scale_tab[32 * q : 32 * q + 8, :].bitcast(I32),
                x_scales[:, 4 * q : 4 * q + 4, :].bitcast(I32),
            )
        nc.sync.dma_start(word_tab[1][:], x_words[1].rearrange("p n t -> p (n t)").bitcast(I32))
        da_sb = sb.tile([P, S], F32, name="da_sb")
        nc.sync.dma_start(da_sb[:], da)
        lt_sb = load_list("lt_sb", lt)
        rt_sb = load_list("rt_sb", rt)

        t1 = sb.tile([P, S], F32, name="t1", tag="t1_slot", align_bytes=64)
        for h in range(HALVES):
            nc.vector.tensor_copy(t1[:, cols(h)], fh_sb[:].indirect(up_sb[:, entries(h)]))
        t2 = sb.tile([P, S], F32, name="t2", tag="w_bf_slot", align_bytes=64)
        for h in range(HALVES):
            nc.vector.tensor_tensor(t2[:, cols(h)], fh_sb[:].indirect(dn_sb[:, entries(h)]), t1[:, cols(h)], SUB)

        def turn(name, src):
            turned = ps.tile([P, 4, P], F32, name=name)
            for b in range(4):
                nc.tensor.transpose(turned[:, b, :], src[:, b : S : 4], ident[:])
            return turned

        fe_ps = turn("fe_ps", fe_sb)
        fc_t = sb.tile([P, 4, P], F32, name="fc_t")
        for b in range(4):
            nc.scalar.activation(fc_t[:, b, :], fe_ps[:, b, :], COPY, scale=ca_col[:, b : b + 1])
        t2_ps = turn("t2_ps", t2)
        t2_t = sb.tile([P, 4, P], F32, name="t2_t")
        nc.scalar.mul(t2_t[:], t2_ps[:], -0.5)
        sum_ps = ps.tile([P, 4, P], F32, name="sum_ps")
        for b in range(4):
            nc.tensor.matmul(sum_ps[:, b, :], lhsT=t2_t[:, b, :], rhs=ident[:], start=True, stop=False, is_transpose=True)
            nc.tensor.matmul(sum_ps[:, b, :], lhsT=fc_t[:, b, :], rhs=ident[:], start=False, stop=True, is_transpose=True)
        t2q = sb.tile([P, S], F32, name="t2q")
        nc.scalar.mul(t2q[:].rearrange("m (p b) -> m p b", b=4), sum_ps[:].rearrange("m b p -> m p b"), -0.5)

        words0 = sb.tile([P, S], U32, name="words0", tag="t1_slot", align_bytes=64)
        nc.vector.tensor_copy(words0[:], word_tab[0][:].bitcast(U32).indirect(offs_sb[:]))
        scales = sb.tile([P, S], U8, name="scales", align_bytes=64)
        nc.vector.tensor_copy(scales[:], scale_tab[:].indirect(offs_sb[:]))

        w_bf = sb.tile([P, PASSES, M, PACK], BF16, name="w_bf", tag="w_bf_slot", align_bytes=64)
        for o in range(PASSES):
            nc.scalar.copy(w_bf[:, o], w_raw[:, o].rearrange("p j m -> p m j"))
        w_codes = sb.tile([P, PASSES * M], U32, name="w_codes", tag="scale_slot", align_bytes=64)
        w_scales = sb.tile([P, PASSES * M], U8, name="w_scales", align_bytes=64)
        nc.vector.quantize_mx(w_codes[:].bitcast(FP8X4), w_scales[:], w_bf[:].rearrange("p o m j -> p (o m j)"))

        words1 = sb.tile([P, S], U32, name="words1", tag="w_bf_slot", align_bytes=64)
        y = [ps.tile([P, HALF], F32, name=f"y{h}") for h in range(HALVES)]
        for h in range(HALVES):
            nc.tensor.matmul_mx(
                y[h][:],
                lhsT=w_codes[:, 0:M].bitcast(FP8X4),
                lhsT_scale=w_scales[:, 0:M],
                rhs=words0[:, cols(h)].bitcast(FP8X4),
                rhs_scale=scales[:, cols(h)],
                start=True,
                stop=False,
            )
        for h in range(HALVES):
            nc.vector.tensor_copy(words1[:, cols(h)], word_tab[1][:].bitcast(U32).indirect(offs_sb[:, entries(h)]))
            nc.tensor.matmul_mx(
                y[h][:],
                lhsT=w_codes[:, M : 2 * M].bitcast(FP8X4),
                lhsT_scale=w_scales[:, M : 2 * M],
                rhs=words1[:, cols(h)].bitcast(FP8X4),
                rhs_scale=scales[4:P, cols(h)],
                start=False,
                stop=True,
            )
        fd = [
            sb.tile([P, HALF], F32, name="fd0", tag="word_slot1"),
            sb.tile([P, HALF], F32, name="fd1", tag="w_bf_slot", align_bytes=64),
        ]
        hn = sb.tile([P, S], F32, name="hn")
        for h in range(HALVES):
            nc.vector.scalar_tensor_tensor(hn[:, cols(h)], y[h][:], 0.2, t2q[:, cols(h)], MULT, ADD)
            nc.vector.tensor_tensor(fd[h][:], fh_sb[:, cols(h)], da_sb[:, cols(h)], MULT)
        u = sb.tile([P, S], F32, name="u")
        for h in range(HALVES):
            nc.vector.tensor_tensor(u[:, cols(h)], hn[:].indirect(lt_sb[:, entries(h)]), fd[h][:], SUB)
        res = [sb.tile([P, HALF], F32, name=f"res{h}") for h in range(HALVES)]
        for h in range(HALVES):
            nc.vector.tensor_tensor(res[h][:], hn[:].indirect(rt_sb[:, entries(h)]), u[:, cols(h)], SUB)
            nc.sync.dma_start(out[:, cols(h)], res[h][:])
